import numpy as np
import ml_dtypes


def mxq(x, axis, fmt="e4m3"):
    dtype, down = {"e4m3": (ml_dtypes.float8_e4m3fn, 7), "e5m2": (ml_dtypes.float8_e5m2, 14)}[fmt]
    v = np.moveaxis(np.asarray(x, np.float32).astype(ml_dtypes.bfloat16).astype(np.float64), axis, -1)
    blocks = v.reshape(v.shape[:-1] + (-1, 32))
    amax = np.abs(blocks).max(-1, keepdims=True)
    byte = np.maximum(np.where(amax > 0, np.frexp(amax)[1] - 1 + 127, 0) - down, 1)
    scale = np.exp2(byte - 127.0)
    codes = (blocks / scale).astype(np.float32).astype(dtype).astype(np.float64)
    return np.moveaxis((codes * scale).reshape(v.shape), -1, axis)


WIDE = False


def mx_kscale(k):
    if not WIDE:
        return np.ones(k)
    levels = np.array([10, -10, 5, -5, 0])
    if k % 512:
        return np.exp2(np.random.permutation(np.resize(levels, k // 32))).repeat(32)
    a = np.empty((k // 512, 16))
    for p in range(k // 512):
        a[p, :8] = np.random.permutation(np.resize(levels, 8))
        for g in range(8):
            far = levels[np.abs(levels - a[p, g]) >= 10]
            a[p, g + 8] = far[np.random.randint(len(far))]
    return np.exp2(a.ravel()).repeat(32)


def f64(x):
    return np.asarray(x).astype(np.float64)


def striped(idx):
    return np.tile(idx.reshape(-1, 16).T, (8, 1)).astype(np.uint16)


def unstriped(offs):
    return offs[:16].T.reshape(-1).astype(np.int64)


def pack_weight(w):
    k, n = w.shape
    w = f64(np.asarray(w, np.float32).astype(ml_dtypes.bfloat16)).reshape(k // 32, 32, n)
    amax = np.abs(w).max(1)
    byte = np.clip(np.where(amax > 0, np.frexp(amax)[1] - 1 + 127 - 7, 1), 1, 254)
    scaled = (w * np.exp2(127.0 - byte)[:, None, :]).reshape(k, n).astype(np.float32)
    words = np.ascontiguousarray(scaled.reshape(k // 512, 128, 4, n).transpose(0, 1, 3, 2)).astype(ml_dtypes.float8_e4m3fn).view(np.uint8)
    return words, np.ascontiguousarray(byte.astype(np.uint8).reshape(k // 512, 16, n))


def unpack_weight(words, scales):
    g, p, n, _ = words.shape
    vals = np.ascontiguousarray(words).view(ml_dtypes.float8_e4m3fn).astype(np.float64) * np.repeat(np.exp2(scales.astype(np.float64) - 127.0), 8, axis=1)[..., None]
    return vals.transpose(0, 1, 3, 2).reshape(g * 512, n)


E2M1 = np.array([0.0, 0.5, 1.0, 1.5, 2.0, 3.0, 4.0, 6.0, -0.0, -0.5, -1.0, -1.5, -2.0, -3.0, -4.0, -6.0])


def pack_fp4(w):
    k, n = w.shape
    w = f64(np.asarray(w, np.float32).astype(ml_dtypes.bfloat16)).reshape(k // 32, 32, n)
    amax = np.abs(w).max(1)
    mant, ex = np.frexp(amax / 6.0)
    byte = np.clip(np.where(amax > 0, np.where(mant > 0.5, ex, ex - 1) + 127, 1), 1, 254)
    scaled = (w * np.exp2(127.0 - byte)[:, None, :]).reshape(k, n).astype(np.float32)
    c = np.ascontiguousarray(scaled.reshape(k // 512, 128, 4, n).transpose(0, 1, 3, 2)).astype(ml_dtypes.float4_e2m1fn).view(np.uint8) & 0xF
    words = (c[..., 0::2] | (c[..., 1::2] << 4)).reshape(k // 512, 128, 2 * n)
    return np.ascontiguousarray(words), np.ascontiguousarray(byte.astype(np.uint8).reshape(k // 512, 16, n))


def unpack_fp4(words, scales):
    g, _, n = scales.shape
    words = np.ascontiguousarray(words).reshape(g, 128, n, 2)
    nib = np.empty((g, 128, n, 4), np.uint8)
    nib[..., 0::2] = words & 0xF
    nib[..., 1::2] = words >> 4
    vals = E2M1[nib] * np.repeat(np.exp2(scales.astype(np.float64) - 127.0), 8, axis=1)[..., None]
    return vals.transpose(0, 1, 3, 2).reshape(g * 512, n)


K, T, S, V, H, N = 512, 2048, 512, 256, 512, 256


def setup_inputs():
    n = np.random.standard_normal
    s = mx_kscale(K)[:, None]
    u = mx_kscale(H)
    near = np.random.permutation(S)
    packed_xT = pack_weight(n((K, T)) * s)
    packed_w2 = pack_fp4(n((H, N)) / np.sqrt(H) / u[:, None])
    packed_w3 = pack_fp4(n((H, N)) / np.sqrt(H) / u[:, None])
    return {
        "x_words": packed_xT[0],
        "x_scales": packed_xT[1],
        "w1": (n((K, H)) / np.sqrt(K) / s * u).astype(np.float32),
        "w2_words": packed_w2[0],
        "w2_scales": packed_w2[1],
        "w3_words": packed_w3[0],
        "w3_scales": packed_w3[1],
        "offs": striped(np.random.permutation(T)[:S]),
        "pos1": striped(near[:V]),
        "pos2": striped(near[V:]),
        "pos3": striped(np.random.permutation(S)[:V]),
    }


def reference(x_words, x_scales, w1, w2_words, w2_scales, w3_words, w3_scales, offs, pos1, pos2, pos3):
    xq = unpack_weight(x_words, x_scales)[:, unstriped(offs)]
    h = mxq(f64(w1), 0, "e4m3").T @ xq
    hq = mxq(h, 0, "e4m3")
    y = unpack_fp4(w3_words, w3_scales).T @ hq
    e = np.exp(unpack_fp4(w2_words, w2_scales).T @ hq)
    e0 = e[:, unstriped(pos1)]
    e1 = e[:, unstriped(pos2)]
    e2 = e[:, unstriped(pos3)]
    num = y[:, unstriped(pos1)] * e0 + y[:, unstriped(pos2)] * e1 + y[:, unstriped(pos3)] * e2
    den = e0 + e1 + e2
    return num / den

@@ -1,0 +1,166 @@
+from contextlib import ExitStack
+
+import concourse.mybir as mybir
+
+K, T, S, V, H, N = 512, 2048, 512, 256, 512, 256
+FLOPS = 2 * K * H * S + 2 * 2 * H * N * S
+
+F32 = mybir.dt.float32
+BF16 = mybir.dt.bfloat16
+I32 = mybir.dt.int32
+U32 = mybir.dt.uint32
+U16 = mybir.dt.uint16
+U8 = mybir.dt.uint8
+FP8X4 = mybir.dt.float8_e4m3fn_x4
+FP4X4 = mybir.dt.float4_e2m1fn_x4
+ACT = mybir.ActivationFunctionType
+ALU = mybir.AluOpType
+
+P = 128
+PACK = 4
+LIST_ROWS = 16
+BLOCK = 128
+HALF = 256
+M_SCALAR = 48
+
+
+def load_scale_rows(queue, plane, rows):
+    for q in range(4):
+        queue.dma_start(out=plane[32 * q : 32 * q + 4, :].bitcast(I32), in_=rows[4 * q : 4 * q + 4, :].bitcast(I32))
+
+
+def tile_picked_zrandla_lin_p_kernel(
+    tc, x_words, x_scales, w1, w2_words, w2_scales, w3_words, w3_scales, offs, pos1, pos2, pos3, out
+):
+    nc = tc.nc
+    with ExitStack() as ctx:
+        keep = ctx.enter_context(tc.tile_pool(name="keep", bufs=1))
+        psum = ctx.enter_context(tc.psum_pool(name="psum", bufs=1))
+
+        offs_t = keep.tile([P, S // LIST_ROWS], U16, name="offs_t")
+        pos_t = [keep.tile([P, V // LIST_ROWS], U16, name=f"pos_t{d}") for d in range(3)]
+        xw = keep.tile([P, T], U32, name="xw", align_bytes=64)
+        xs = keep.tile([P, T], U8, name="xs", align_bytes=64)
+        w1_raw = keep.tile([P, PACK, H], F32, name="w1_raw", align_bytes=64)
+        w23_words = [keep.tile([P, 2 * N], U8, name=f"w23_words{i}", align_bytes=64) for i in range(2)]
+        w23_scales = [keep.tile([P, N], U8, name=f"w23_scales{i}", align_bytes=64) for i in range(2)]
+
+        nc.gpsimd.memset(xs[:, : T // 2].bitcast(I32), 0)
+        nc.vector.memset(xs[:, T // 2 :].bitcast(I32), 0)
+        for plane in w23_scales:
+            nc.gpsimd.memset(plane[:].bitcast(I32), 0)
+
+        nc.sync.dma_start(out=w1_raw[:], in_=w1.rearrange("(p j) c -> p j c", j=PACK))
+        load_scale_rows(nc.scalar, xs, x_scales[0])
+        nc.sync.dma_start(offs_t[:], offs)
+        nc.sync.dma_start(out=xw[:].bitcast(I32), in_=x_words[0].rearrange("p n t -> p (n t)").bitcast(I32))
+        nc.sync.dma_start(out=w23_words[0][:].bitcast(I32), in_=w2_words[0].bitcast(I32))
+        load_scale_rows(nc.sync, w23_scales[0], w2_scales[0])
+        nc.sync.dma_start(out=w23_words[1][:].bitcast(I32), in_=w3_words[0].bitcast(I32))
+        for tile, src in zip(pos_t, (pos1, pos2, pos3)):
+            nc.sync.dma_start(tile[:], src)
+        load_scale_rows(nc.sync, w23_scales[1], w3_scales[0])
+
+        w1_bf = keep.tile([P, PACK * H], BF16, name="w1_bf", align_bytes=64)
+        dst = w1_bf[:].rearrange("p (t m j) -> p m t j", t=PACK, j=PACK)
+        src = w1_raw[:].rearrange("p j (m t) -> p m t j", t=PACK)
+        nc.scalar.copy(out=dst[:, :M_SCALAR], in_=src[:, :M_SCALAR])
+        nc.vector.tensor_copy(out=dst[:, M_SCALAR:], in_=src[:, M_SCALAR:])
+        w1_codes = keep.tile([P, H], U32, name="w1_codes", align_bytes=64)
+        w1_scales = keep.tile([P, H], U8, name="w1_scales", align_bytes=64)
+        nc.vector.quantize_mx(out=w1_codes[:].bitcast(FP8X4), scales=w1_scales[:], in_=w1_bf[:])
+
+        xg_scales = keep.tile([P, S], U8, name="xg_scales", align_bytes=64)
+        nc.vector.tensor_copy(xg_scales[:], xs[:].indirect(offs_t[:]))
+        xg_words = []
+        for a in range(S // HALF):
+            g = keep.tile([P, HALF], U32, name=f"xg_words{a}", align_bytes=64)
+            cols = HALF // LIST_ROWS
+            nc.vector.tensor_copy(g[:], xw[:].indirect(offs_t[:, a * cols : (a + 1) * cols]))
+            xg_words.append(g)
+
+        h_codes = keep.tile([P, S], U32, name="h_codes", align_bytes=64)
+        h_scales = keep.tile([P, S], U8, name="h_scales", align_bytes=64)
+        h_bf = []
+        for b in range(S // BLOCK):
+            bank = psum.tile([P, PACK, BLOCK], F32, name=f"h_bank{b}")
+            a, o = divmod(b * BLOCK, HALF)
+            for t in range(PACK):
+                cols = slice(t * P, (t + 1) * P)
+                nc.tensor.matmul_mx(
+                    out=bank[:, t, :],
+                    lhsT=w1_codes[:, cols].bitcast(FP8X4),
+                    lhsT_scale=w1_scales[:, cols],
+                    rhs=xg_words[a][:, o : o + BLOCK].bitcast(FP8X4),
+                    rhs_scale=xg_scales[:, b * BLOCK : (b + 1) * BLOCK],
+                    start=True,
+                    stop=True,
+                )
+            hb = keep.tile([P, BLOCK, PACK], BF16, name=f"h_bf{b}", align_bytes=64)
+            if b % 2 == 0:
+                nc.scalar.copy(out=hb[:], in_=bank[:].rearrange("p t n -> p n t"))
+            else:
+                nc.vector.tensor_copy(out=hb[:], in_=bank[:].rearrange("p t n -> p n t"))
+            h_bf.append(hb)
+        for b in range(S // BLOCK):
+            cols = slice(b * BLOCK, (b + 1) * BLOCK)
+            nc.vector.quantize_mx(
+                out=h_codes[:, cols].bitcast(FP8X4),
+                scales=h_scales[:, cols],
+                in_=h_bf[b][:].rearrange("p n t -> p (n t)"),
+            )
+
+        def second_product(acc, which, mt, cols):
+            nc.tensor.matmul_mx(
+                out=acc,
+                lhsT=w23_words[which][:, 2 * P * mt : 2 * P * (mt + 1)].bitcast(FP4X4),
+                lhsT_scale=w23_scales[which][:, P * mt : P * (mt + 1)],
+                rhs=h_codes[:, cols].bitcast(FP8X4),
+                rhs_scale=h_scales[:, cols],
+                start=True,
+                stop=True,
+            )
+
+        e = [keep.tile([P, S], F32, name=f"e{mt}") for mt in range(2)]
+        ye = [keep.tile([P, S], F32, name=f"ye{mt}") for mt in range(2)]
+        last = S - BLOCK
+        s0_head = psum.tile([P, last], F32, name="s0_head")
+        s0_tail = psum.tile([P, BLOCK], F32, name="s0_tail")
+        y0 = psum.tile([P, S], F32, name="y0")
+        s1 = psum.tile([P, S], F32, name="s1")
+        y1 = psum.tile([P, S], F32, name="y1", tag="h_bank0")
+        for b in range(last // BLOCK):
+            cols = slice(b * BLOCK, (b + 1) * BLOCK)
+            second_product(s0_head[:, cols], 0, 0, cols)
+        nc.scalar.activation(out=e[0][:, :last], in_=s0_head[:], func=ACT.Exp)
+        second_product(s0_tail[:], 0, 0, slice(last, S))
+        nc.scalar.activation(out=e[0][:, last:], in_=s0_tail[:], func=ACT.Exp)
+        second_product(y0[:], 1, 0, slice(0, S))
+        second_product(s1[:], 0, 1, slice(0, S))
+        nc.scalar.activation(out=e[1][:], in_=s1[:], func=ACT.Exp)
+        second_product(y1[:], 1, 1, slice(0, S))
+        y = [y0, y1]
+
+        def part(name, window, d, prev):
+            acc = keep.tile([P, V], F32, name=name)
+            if prev is None:
+                nc.vector.tensor_copy(acc[:], window[:].indirect(pos_t[d][:]))
+            else:
+                nc.vector.tensor_tensor(acc[:], window[:].indirect(pos_t[d][:]), prev[:], ALU.add)
+            return acc
+
+        for mt in range(2):
+            den = part(f"den{mt}0", e[mt], 0, None)
+            nc.vector.tensor_tensor(ye[mt][:], y[mt][:], e[mt][:], ALU.mult)
+            den = part(f"den{mt}1", e[mt], 1, den)
+            num = part(f"num{mt}0", ye[mt], 0, None)
+            den = part(f"den{mt}2", e[mt], 2, den)
+            num = part(f"num{mt}1", ye[mt], 1, num)
+            root = keep.tile([P, V], F32, name=f"root{mt}")
+            nc.scalar.activation(out=root[:], in_=den[:], func=ACT.Abs_reciprocal_sqrt)
+            inv = keep.tile([P, V], F32, name=f"inv{mt}")
+            nc.scalar.activation(out=inv[:], in_=root[:], func=ACT.Square)
+            num = part(f"num{mt}2", ye[mt], 2, num)
+            res = keep.tile([P, V], F32, name=f"res{mt}")
+            nc.vector.tensor_tensor(res[:], num[:], inv[:], ALU.mult)
+            nc.sync.dma_start(out=out[mt * P : (mt + 1) * P, :], in_=res[:])

@@ -21,7 +21,7 @@ PACK = 4
 LIST_ROWS = 16
 BLOCK = 128
 HALF = 256
-M_SCALAR = 48
+M_SCALAR = 80
 
 
 def load_scale_rows(queue, plane, rows):
@@ -45,13 +45,12 @@ def tile_picked_zrandla_lin_p_kernel(
         w23_words = [keep.tile([P, 2 * N], U8, name=f"w23_words{i}", align_bytes=64) for i in range(2)]
         w23_scales = [keep.tile([P, N], U8, name=f"w23_scales{i}", align_bytes=64) for i in range(2)]
 
-        nc.gpsimd.memset(xs[:, : T // 2].bitcast(I32), 0)
-        nc.vector.memset(xs[:, T // 2 :].bitcast(I32), 0)
+        nc.gpsimd.memset(xs[:].bitcast(I32), 0)
         for plane in w23_scales:
             nc.gpsimd.memset(plane[:].bitcast(I32), 0)
 
         nc.sync.dma_start(out=w1_raw[:], in_=w1.rearrange("(p j) c -> p j c", j=PACK))
-        load_scale_rows(nc.scalar, xs, x_scales[0])
+        load_scale_rows(nc.sync, xs, x_scales[0])
         nc.sync.dma_start(offs_t[:], offs)
         nc.sync.dma_start(out=xw[:].bitcast(I32), in_=x_words[0].rearrange("p n t -> p (n t)").bitcast(I32))
         nc.sync.dma_start(out=w23_words[0][:].bitcast(I32), in_=w2_words[0].bitcast(I32))
@@ -66,12 +65,12 @@ def tile_picked_zrandla_lin_p_kernel(
         src = w1_raw[:].rearrange("p j (m t) -> p m t j", t=PACK)
         nc.scalar.copy(out=dst[:, :M_SCALAR], in_=src[:, :M_SCALAR])
         nc.vector.tensor_copy(out=dst[:, M_SCALAR:], in_=src[:, M_SCALAR:])
+        xg_scales = keep.tile([P, S], U8, name="xg_scales", align_bytes=64)
+        nc.vector.tensor_copy(xg_scales[:], xs[:].indirect(offs_t[:]))
         w1_codes = keep.tile([P, H], U32, name="w1_codes", align_bytes=64)
         w1_scales = keep.tile([P, H], U8, name="w1_scales", align_bytes=64)
         nc.vector.quantize_mx(out=w1_codes[:].bitcast(FP8X4), scales=w1_scales[:], in_=w1_bf[:])
 
-        xg_scales = keep.tile([P, S], U8, name="xg_scales", align_bytes=64)
-        nc.vector.tensor_copy(xg_scales[:], xs[:].indirect(offs_t[:]))
         xg_words = []
         for a in range(S // HALF):
             g = keep.tile([P, HALF], U32, name=f"xg_words{a}", align_bytes=64)
@@ -97,7 +96,7 @@ def tile_picked_zrandla_lin_p_kernel(
                     stop=True,
                 )
             hb = keep.tile([P, BLOCK, PACK], BF16, name=f"h_bf{b}", align_bytes=64)
-            if b % 2 == 0:
+            if b != 1:
                 nc.scalar.copy(out=hb[:], in_=bank[:].rearrange("p t n -> p n t"))
             else:
                 nc.vector.tensor_copy(out=hb[:], in_=bank[:].rearrange("p t n -> p n t"))
@@ -129,9 +128,8 @@ def tile_picked_zrandla_lin_p_kernel(
         y0 = psum.tile([P, S], F32, name="y0")
         s1 = psum.tile([P, S], F32, name="s1")
         y1 = psum.tile([P, S], F32, name="y1", tag="h_bank0")
-        for b in range(last // BLOCK):
-            cols = slice(b * BLOCK, (b + 1) * BLOCK)
-            second_product(s0_head[:, cols], 0, 0, cols)
+        second_product(s0_head[:, :HALF], 0, 0, slice(0, HALF))
+        second_product(s0_head[:, HALF:], 0, 0, slice(HALF, last))
         nc.scalar.activation(out=e[0][:, :last], in_=s0_head[:], func=ACT.Exp)
         second_product(s0_tail[:], 0, 0, slice(last, S))
         nc.scalar.activation(out=e[0][:, last:], in_=s0_tail[:], func=ACT.Exp)
@@ -160,7 +158,12 @@ def tile_picked_zrandla_lin_p_kernel(
             nc.scalar.activation(out=root[:], in_=den[:], func=ACT.Abs_reciprocal_sqrt)
             inv = keep.tile([P, V], F32, name=f"inv{mt}")
             nc.scalar.activation(out=inv[:], in_=root[:], func=ACT.Square)
-            num = part(f"num{mt}2", ye[mt], 2, num)
-            res = keep.tile([P, V], F32, name=f"res{mt}")
-            nc.vector.tensor_tensor(res[:], num[:], inv[:], ALU.mult)
-            nc.sync.dma_start(out=out[mt * P : (mt + 1) * P, :], in_=res[:])
+            for a in range(mt + 1):
+                width = V // (mt + 1)
+                cols = slice(a * width, (a + 1) * width)
+                entries = slice(cols.start // LIST_ROWS, cols.stop // LIST_ROWS)
+                total = keep.tile([P, width], F32, name=f"total{mt}{a}")
+                nc.vector.tensor_tensor(total[:], ye[mt][:].indirect(pos_t[2][:, entries]), num[:, cols], ALU.add)
+                res = keep.tile([P, width], F32, name=f"res{mt}{a}")
+                nc.vector.tensor_tensor(res[:], total[:], inv[:, cols], ALU.mult)
+                nc.sync.dma_start(out=out[mt * P : (mt + 1) * P, cols], in_=res[:])

@@ -56,9 +56,10 @@ def tile_picked_zrandla_lin_p_kernel(
         nc.sync.dma_start(out=w23_words[0][:].bitcast(I32), in_=w2_words[0].bitcast(I32))
         load_scale_rows(nc.sync, w23_scales[0], w2_scales[0])
         nc.sync.dma_start(out=w23_words[1][:].bitcast(I32), in_=w3_words[0].bitcast(I32))
-        for tile, src in zip(pos_t, (pos1, pos2, pos3)):
-            nc.sync.dma_start(tile[:], src)
+        nc.sync.dma_start(pos_t[0][:], pos1)
         load_scale_rows(nc.sync, w23_scales[1], w3_scales[0])
+        nc.sync.dma_start(pos_t[1][:], pos2)
+        nc.sync.dma_start(pos_t[2][:], pos3)
 
         w1_bf = keep.tile([P, PACK * H], BF16, name="w1_bf", align_bytes=64)
         dst = w1_bf[:].rearrange("p (t m j) -> p m t j", t=PACK, j=PACK)
@@ -121,7 +122,7 @@ def tile_picked_zrandla_lin_p_kernel(
             )
 
         e = [keep.tile([P, S], F32, name=f"e{mt}") for mt in range(2)]
-        ye = [keep.tile([P, S], F32, name=f"ye{mt}") for mt in range(2)]
+        ye0 = keep.tile([P, S], F32, name="ye0")
         last = S - BLOCK
         s0_head = psum.tile([P, last], F32, name="s0_head")
         s0_tail = psum.tile([P, BLOCK], F32, name="s0_tail")
@@ -137,33 +138,51 @@ def tile_picked_zrandla_lin_p_kernel(
         second_product(s1[:], 0, 1, slice(0, S))
         nc.scalar.activation(out=e[1][:], in_=s1[:], func=ACT.Exp)
         second_product(y1[:], 1, 1, slice(0, S))
-        y = [y0, y1]
+        y1_sb = keep.tile([P, S], F32, name="y1_sb")
+        nc.scalar.copy(out=y1_sb[:], in_=y1[:])
 
-        def part(name, window, d, prev):
-            acc = keep.tile([P, V], F32, name=name)
+        def fetch(name, window, entries, prev=None, tag=None):
+            acc = keep.tile([P, LIST_ROWS * entries.shape[1]], F32, name=name, tag=tag or name)
             if prev is None:
-                nc.vector.tensor_copy(acc[:], window[:].indirect(pos_t[d][:]))
+                nc.vector.tensor_copy(acc[:], window[:].indirect(entries))
             else:
-                nc.vector.tensor_tensor(acc[:], window[:].indirect(pos_t[d][:]), prev[:], ALU.add)
+                nc.vector.tensor_tensor(acc[:], window[:].indirect(entries), prev, ALU.add)
             return acc
 
-        for mt in range(2):
-            den = part(f"den{mt}0", e[mt], 0, None)
-            nc.vector.tensor_tensor(ye[mt][:], y[mt][:], e[mt][:], ALU.mult)
-            den = part(f"den{mt}1", e[mt], 1, den)
-            num = part(f"num{mt}0", ye[mt], 0, None)
-            den = part(f"den{mt}2", e[mt], 2, den)
-            num = part(f"num{mt}1", ye[mt], 1, num)
+        def inverse(mt, den):
             root = keep.tile([P, V], F32, name=f"root{mt}")
             nc.scalar.activation(out=root[:], in_=den[:], func=ACT.Abs_reciprocal_sqrt)
             inv = keep.tile([P, V], F32, name=f"inv{mt}")
             nc.scalar.activation(out=inv[:], in_=root[:], func=ACT.Square)
-            for a in range(mt + 1):
-                width = V // (mt + 1)
-                cols = slice(a * width, (a + 1) * width)
-                entries = slice(cols.start // LIST_ROWS, cols.stop // LIST_ROWS)
-                total = keep.tile([P, width], F32, name=f"total{mt}{a}")
-                nc.vector.tensor_tensor(total[:], ye[mt][:].indirect(pos_t[2][:, entries]), num[:, cols], ALU.add)
-                res = keep.tile([P, width], F32, name=f"res{mt}{a}")
-                nc.vector.tensor_tensor(res[:], total[:], inv[:, cols], ALU.mult)
-                nc.sync.dma_start(out=out[mt * P : (mt + 1) * P, cols], in_=res[:])
+            return inv
+
+        def finish(mt, cols, total, inv):
+            res = keep.tile([P, cols.stop - cols.start], F32, name=f"res{mt}_{cols.start}")
+            nc.vector.tensor_tensor(res[:], total[:], inv[:, cols], ALU.mult)
+            nc.sync.dma_start(out=out[mt * P : (mt + 1) * P, cols], in_=res[:])
+
+        p0, p1, p2 = (t[:] for t in pos_t)
+        den00 = fetch("den00", e[0], p0, tag="den00_then_ye1")
+        nc.vector.tensor_tensor(ye0[:], y0[:], e[0][:], ALU.mult)
+        den01 = fetch("den01", e[0], p1, den00[:])
+        ye1 = keep.tile([P, S], F32, name="ye1", tag="den00_then_ye1")
+        nc.gpsimd.tensor_tensor(ye1[:], y1_sb[:], e[1][:], ALU.mult)
+        den10 = fetch("den10", e[1], p1)
+        num00 = fetch("num00", ye0, p1)
+        den11 = fetch("den11", e[1], p0, den10[:])
+        num01 = fetch("num01", ye0, p0, num00[:])
+        den02 = fetch("den02", e[0], p2, den01[:])
+        inv0 = inverse(0, den02)
+        num02 = fetch("num02", ye0, p2, num01[:])
+        den12 = fetch("den12", e[1], p2, den11[:])
+        inv1 = inverse(1, den12)
+        finish(0, slice(0, V), num02, inv0)
+        halves = [slice(a * V // 2, (a + 1) * V // 2) for a in range(2)]
+        entries = [slice(c.start // LIST_ROWS, c.stop // LIST_ROWS) for c in halves]
+        num1 = [None, None]
+        for d in range(3):
+            for a in range(2):
+                prev = None if d == 0 else num1[a][:]
+                num1[a] = fetch(f"num1{d}_{a}", ye1, pos_t[d][:, entries[a]], prev)
+        for a in range(2):
+            finish(1, halves[a], num1[a], inv1)

@@ -1,6 +1,7 @@
 from contextlib import ExitStack
 
 import concourse.mybir as mybir
+from concourse.masks import make_identity
 
 K, T, S, V, H, N = 512, 2048, 512, 256, 512, 256
 FLOPS = 2 * K * H * S + 2 * 2 * H * N * S
@@ -21,7 +22,8 @@ PACK = 4
 LIST_ROWS = 16
 BLOCK = 128
 HALF = 256
-M_SCALAR = 80
+M_HALF = P // 2
+M_SCALAR_LATE = 22
 
 
 def load_scale_rows(queue, plane, rows):
@@ -41,33 +43,38 @@ def tile_picked_zrandla_lin_p_kernel(
         pos_t = [keep.tile([P, V // LIST_ROWS], U16, name=f"pos_t{d}") for d in range(3)]
         xw = keep.tile([P, T], U32, name="xw", align_bytes=64)
         xs = keep.tile([P, T], U8, name="xs", align_bytes=64)
-        w1_raw = keep.tile([P, PACK, H], F32, name="w1_raw", align_bytes=64)
+        w1_raw = [keep.tile([P, PACK, H // 2], F32, name=f"w1_raw{a}", align_bytes=64) for a in range(2)]
         w23_words = [keep.tile([P, 2 * N], U8, name=f"w23_words{i}", align_bytes=64) for i in range(2)]
         w23_scales = [keep.tile([P, N], U8, name=f"w23_scales{i}", align_bytes=64) for i in range(2)]
 
         nc.gpsimd.memset(xs[:].bitcast(I32), 0)
         for plane in w23_scales:
             nc.gpsimd.memset(plane[:].bitcast(I32), 0)
+        ident = keep.tile([P, P], F32, name="ident")
+        make_identity(nc, ident[:])
 
-        nc.sync.dma_start(out=w1_raw[:], in_=w1.rearrange("(p j) c -> p j c", j=PACK))
+        w1_rows = w1.rearrange("(p j) c -> p j c", j=PACK)
+        nc.sync.dma_start(out=w1_raw[0][:], in_=w1_rows[:, :, : H // 2])
         load_scale_rows(nc.sync, xs, x_scales[0])
         nc.sync.dma_start(offs_t[:], offs)
+        nc.sync.dma_start(out=w1_raw[1][:], in_=w1_rows[:, :, H // 2 :])
         nc.sync.dma_start(out=xw[:].bitcast(I32), in_=x_words[0].rearrange("p n t -> p (n t)").bitcast(I32))
         nc.sync.dma_start(out=w23_words[0][:].bitcast(I32), in_=w2_words[0].bitcast(I32))
         load_scale_rows(nc.sync, w23_scales[0], w2_scales[0])
         nc.sync.dma_start(out=w23_words[1][:].bitcast(I32), in_=w3_words[0].bitcast(I32))
-        nc.sync.dma_start(pos_t[0][:], pos1)
         load_scale_rows(nc.sync, w23_scales[1], w3_scales[0])
+        nc.sync.dma_start(pos_t[0][:], pos1)
         nc.sync.dma_start(pos_t[1][:], pos2)
         nc.sync.dma_start(pos_t[2][:], pos3)
 
         w1_bf = keep.tile([P, PACK * H], BF16, name="w1_bf", align_bytes=64)
         dst = w1_bf[:].rearrange("p (t m j) -> p m t j", t=PACK, j=PACK)
-        src = w1_raw[:].rearrange("p j (m t) -> p m t j", t=PACK)
-        nc.scalar.copy(out=dst[:, :M_SCALAR], in_=src[:, :M_SCALAR])
-        nc.vector.tensor_copy(out=dst[:, M_SCALAR:], in_=src[:, M_SCALAR:])
+        src = [raw[:].rearrange("p j (m t) -> p m t j", t=PACK) for raw in w1_raw]
+        nc.scalar.copy(out=dst[:, :M_HALF], in_=src[0])
+        nc.scalar.copy(out=dst[:, M_HALF : M_HALF + M_SCALAR_LATE], in_=src[1][:, :M_SCALAR_LATE])
         xg_scales = keep.tile([P, S], U8, name="xg_scales", align_bytes=64)
         nc.vector.tensor_copy(xg_scales[:], xs[:].indirect(offs_t[:]))
+        nc.vector.tensor_copy(out=dst[:, M_HALF + M_SCALAR_LATE :], in_=src[1][:, M_SCALAR_LATE:])
         w1_codes = keep.tile([P, H], U32, name="w1_codes", align_bytes=64)
         w1_scales = keep.tile([P, H], U8, name="w1_scales", align_bytes=64)
         nc.vector.quantize_mx(out=w1_codes[:].bitcast(FP8X4), scales=w1_scales[:], in_=w1_bf[:])
@@ -122,7 +129,6 @@ def tile_picked_zrandla_lin_p_kernel(
             )
 
         e = [keep.tile([P, S], F32, name=f"e{mt}") for mt in range(2)]
-        ye0 = keep.tile([P, S], F32, name="ye0")
         last = S - BLOCK
         s0_head = psum.tile([P, last], F32, name="s0_head")
         s0_tail = psum.tile([P, BLOCK], F32, name="s0_tail")
@@ -138,21 +144,19 @@ def tile_picked_zrandla_lin_p_kernel(
         second_product(s1[:], 0, 1, slice(0, S))
         nc.scalar.activation(out=e[1][:], in_=s1[:], func=ACT.Exp)
         second_product(y1[:], 1, 1, slice(0, S))
-        y1_sb = keep.tile([P, S], F32, name="y1_sb")
-        nc.scalar.copy(out=y1_sb[:], in_=y1[:])
 
-        def fetch(name, window, entries, prev=None, tag=None):
+        def fetch(name, window, entries, prev=None, op=ALU.add, tag=None):
             acc = keep.tile([P, LIST_ROWS * entries.shape[1]], F32, name=name, tag=tag or name)
             if prev is None:
                 nc.vector.tensor_copy(acc[:], window[:].indirect(entries))
             else:
-                nc.vector.tensor_tensor(acc[:], window[:].indirect(entries), prev, ALU.add)
+                nc.vector.tensor_tensor(acc[:], window[:].indirect(entries), prev, op)
             return acc
 
         def inverse(mt, den):
-            root = keep.tile([P, V], F32, name=f"root{mt}")
-            nc.scalar.activation(out=root[:], in_=den[:], func=ACT.Abs_reciprocal_sqrt)
-            inv = keep.tile([P, V], F32, name=f"inv{mt}")
+            root = keep.tile([P, V], F32, name=f"root{mt}", tag="root")
+            nc.scalar.activation(out=root[:], in_=den, func=ACT.Abs_reciprocal_sqrt)
+            inv = keep.tile([P, V], F32, name=f"inv{mt}", tag=f"inv{mt}")
             nc.scalar.activation(out=inv[:], in_=root[:], func=ACT.Square)
             return inv
 
@@ -161,28 +165,59 @@ def tile_picked_zrandla_lin_p_kernel(
             nc.vector.tensor_tensor(res[:], total[:], inv[:, cols], ALU.mult)
             nc.sync.dma_start(out=out[mt * P : (mt + 1) * P, cols], in_=res[:])
 
-        p0, p1, p2 = (t[:] for t in pos_t)
-        den00 = fetch("den00", e[0], p0, tag="den00_then_ye1")
-        nc.vector.tensor_tensor(ye0[:], y0[:], e[0][:], ALU.mult)
-        den01 = fetch("den01", e[0], p1, den00[:])
-        ye1 = keep.tile([P, S], F32, name="ye1", tag="den00_then_ye1")
-        nc.gpsimd.tensor_tensor(ye1[:], y1_sb[:], e[1][:], ALU.mult)
-        den10 = fetch("den10", e[1], p1)
-        num00 = fetch("num00", ye0, p1)
-        den11 = fetch("den11", e[1], p0, den10[:])
-        num01 = fetch("num01", ye0, p0, num00[:])
-        den02 = fetch("den02", e[0], p2, den01[:])
-        inv0 = inverse(0, den02)
-        num02 = fetch("num02", ye0, p2, num01[:])
-        den12 = fetch("den12", e[1], p2, den11[:])
-        inv1 = inverse(1, den12)
-        finish(0, slice(0, V), num02, inv0)
         halves = [slice(a * V // 2, (a + 1) * V // 2) for a in range(2)]
         entries = [slice(c.start // LIST_ROWS, c.stop // LIST_ROWS) for c in halves]
-        num1 = [None, None]
-        for d in range(3):
+
+        def add_turned(acc, src, d):
+            nc.tensor.matmul(acc, lhsT=src, rhs=ident[:], is_transpose=True, start=(d == 0), stop=(d == 2))
+
+        y0_sb = keep.tile([P, S], F32, name="y0_sb")
+        nc.scalar.copy(out=y0_sb[:], in_=y0[:])
+        num0_t = [psum.tile([P, P], F32, name=f"num0_t{a}", tag=f"h_bank{2 + a}") for a in range(2)]
+        den0_t = psum.tile([P, V], F32, name="den0_t", tag="h_bank1")
+
+        def product(d, weights):
+            prod = fetch(f"prod0{d}", y0_sb, pos_t[d][:], weights[:], op=ALU.mult)
             for a in range(2):
-                prev = None if d == 0 else num1[a][:]
-                num1[a] = fetch(f"num1{d}_{a}", ye1, pos_t[d][:, entries[a]], prev)
+                add_turned(num0_t[a][:], prod[:, halves[a]], d)
+
+        e00 = fetch("e00", e[0], pos_t[0][:])
+        den10 = fetch("den10", e[1], pos_t[0][:], tag="den10_then_ye1")
+        product(0, e00)
+        e01 = fetch("e01", e[0], pos_t[1][:])
+        den11 = fetch("den11", e[1], pos_t[1][:], den10[:])
+        product(1, e01)
+        e02 = fetch("e02", e[0], pos_t[2][:])
         for a in range(2):
-            finish(1, halves[a], num1[a], inv1)
+            for d, part in enumerate((e00, e01, e02)):
+                add_turned(den0_t[:, halves[a]], part[:, halves[a]], d)
+        root0_t = keep.tile([P, V], F32, name="root0_t", tag="root")
+        nc.scalar.activation(out=root0_t[:], in_=den0_t[:], func=ACT.Abs_reciprocal_sqrt)
+        inv0_t = [keep.tile([P, P], F32, name=f"inv0_t{a}", tag=f"inv0_t{a}") for a in range(2)]
+        for a in range(2):
+            nc.scalar.activation(out=inv0_t[a][:], in_=root0_t[:, halves[a]], func=ACT.Square)
+        ye1 = keep.tile([P, S], F32, name="ye1", tag="den10_then_ye1")
+        nc.vector.tensor_tensor(ye1[:], y1[:], e[1][:], ALU.mult)
+        product(2, e02)
+        num10 = fetch("num10", ye1, pos_t[0][:])
+        den12 = fetch("den12", e[1], pos_t[2][:], den11[:])
+        inv1 = inverse(1, den12[:])
+
+        res0_t = keep.tile([P, V], F32, name="res0_t")
+        res0_back = psum.tile([P, V], F32, name="res0_back", tag="s0_head")
+        for a in range(2):
+            nc.vector.tensor_tensor(res0_t[:, halves[a]], num0_t[a][:], inv0_t[a][:], ALU.mult)
+        for a in range(2):
+            nc.tensor.transpose(res0_back[:, halves[a]], res0_t[:, halves[a]], ident[:])
+        res0 = keep.tile([P, V], F32, name="res0")
+        nc.scalar.copy(out=res0[:], in_=res0_back[:])
+        nc.sync.dma_start(out=out[:P, :], in_=res0[:])
+
+        num11 = keep.tile([P, V], F32, name="num11", tag="inv0_t0")
+        for a in range(2):
+            nc.vector.tensor_tensor(
+                num11[:, halves[a]], ye1[:].indirect(pos_t[1][:, entries[a]]), num10[:, halves[a]], ALU.add
+            )
+        num12 = [fetch(f"num12_{a}", ye1, pos_t[2][:, entries[a]], num11[:, halves[a]]) for a in range(2)]
+        for a in range(2):
+            finish(1, halves[a], num12[a], inv1)

@@ -79,6 +79,18 @@ def tile_picked_zrandla_lin_p_kernel(
         w1_scales = keep.tile([P, H], U8, name="w1_scales", align_bytes=64)
         nc.vector.quantize_mx(out=w1_codes[:].bitcast(FP8X4), scales=w1_scales[:], in_=w1_bf[:])
 
+        s1 = psum.tile([P, S], F32, name="s1")
+        for t in range(2):
+            nc.tensor.matmul_mx(
+                out=s1[:],
+                lhsT=w1_codes[:, t * P : (t + 1) * P].bitcast(FP8X4),
+                lhsT_scale=w1_scales[:, t * P : (t + 1) * P],
+                rhs=w1_codes[:].bitcast(FP8X4),
+                rhs_scale=w1_scales[:],
+                start=True,
+                stop=True,
+            )
+
         xg_words = []
         for a in range(S // HALF):
             g = keep.tile([P, HALF], U32, name=f"xg_words{a}", align_bytes=64)
@@ -133,7 +145,6 @@ def tile_picked_zrandla_lin_p_kernel(
         s0_head = psum.tile([P, last], F32, name="s0_head")
         s0_tail = psum.tile([P, BLOCK], F32, name="s0_tail")
         y0 = psum.tile([P, S], F32, name="y0")
-        s1 = psum.tile([P, S], F32, name="s1")
         y1 = psum.tile([P, S], F32, name="y1", tag="h_bank0")
         second_product(s0_head[:, :HALF], 0, 0, slice(0, HALF))
         second_product(s0_head[:, HALF:], 0, 0, slice(HALF, last))

@@ -23,7 +23,7 @@ LIST_ROWS = 16
 BLOCK = 128
 HALF = 256
 M_HALF = P // 2
-M_SCALAR_LATE = 22
+M_SCALAR = 22
 
 
 def load_scale_rows(queue, plane, rows):
@@ -55,9 +55,9 @@ def tile_picked_zrandla_lin_p_kernel(
 
         w1_rows = w1.rearrange("(p j) c -> p j c", j=PACK)
         nc.sync.dma_start(out=w1_raw[0][:], in_=w1_rows[:, :, : H // 2])
+        nc.sync.dma_start(out=w1_raw[1][:], in_=w1_rows[:, :, H // 2 :])
         load_scale_rows(nc.sync, xs, x_scales[0])
         nc.sync.dma_start(offs_t[:], offs)
-        nc.sync.dma_start(out=w1_raw[1][:], in_=w1_rows[:, :, H // 2 :])
         nc.sync.dma_start(out=xw[:].bitcast(I32), in_=x_words[0].rearrange("p n t -> p (n t)").bitcast(I32))
         nc.sync.dma_start(out=w23_words[0][:].bitcast(I32), in_=w2_words[0].bitcast(I32))
         load_scale_rows(nc.sync, w23_scales[0], w2_scales[0])
@@ -70,14 +70,15 @@ def tile_picked_zrandla_lin_p_kernel(
         w1_bf = keep.tile([P, PACK * H], BF16, name="w1_bf", align_bytes=64)
         dst = w1_bf[:].rearrange("p (t m j) -> p m t j", t=PACK, j=PACK)
         src = [raw[:].rearrange("p j (m t) -> p m t j", t=PACK) for raw in w1_raw]
-        nc.scalar.copy(out=dst[:, :M_HALF], in_=src[0])
-        nc.scalar.copy(out=dst[:, M_HALF : M_HALF + M_SCALAR_LATE], in_=src[1][:, :M_SCALAR_LATE])
-        xg_scales = keep.tile([P, S], U8, name="xg_scales", align_bytes=64)
-        nc.vector.tensor_copy(xg_scales[:], xs[:].indirect(offs_t[:]))
-        nc.vector.tensor_copy(out=dst[:, M_HALF + M_SCALAR_LATE :], in_=src[1][:, M_SCALAR_LATE:])
+        for a in range(2):
+            m0 = a * M_HALF
+            nc.scalar.copy(out=dst[:, m0 : m0 + M_SCALAR], in_=src[a][:, :M_SCALAR])
+            nc.vector.tensor_copy(out=dst[:, m0 + M_SCALAR : m0 + M_HALF], in_=src[a][:, M_SCALAR:])
         w1_codes = keep.tile([P, H], U32, name="w1_codes", align_bytes=64)
         w1_scales = keep.tile([P, H], U8, name="w1_scales", align_bytes=64)
         nc.vector.quantize_mx(out=w1_codes[:].bitcast(FP8X4), scales=w1_scales[:], in_=w1_bf[:])
+        xg_scales = keep.tile([P, S], U8, name="xg_scales", align_bytes=64)
+        nc.vector.tensor_copy(xg_scales[:], xs[:].indirect(offs_t[:]))
 
         s1 = psum.tile([P, S], F32, name="s1")
         for t in range(2):

@@ -22,8 +22,8 @@ PACK = 4
 LIST_ROWS = 16
 BLOCK = 128
 HALF = 256
+PIECE = 128
 M_HALF = P // 2
-M_SCALAR = 22
 
 
 def load_scale_rows(queue, plane, rows):
@@ -48,6 +48,8 @@ def tile_picked_zrandla_lin_p_kernel(
         w23_scales = [keep.tile([P, N], U8, name=f"w23_scales{i}", align_bytes=64) for i in range(2)]
 
         nc.gpsimd.memset(xs[:].bitcast(I32), 0)
+        xg_scales = keep.tile([P, S], U8, name="xg_scales", align_bytes=64)
+        nc.gpsimd.memset(xg_scales[:].bitcast(I32), 0)
         for plane in w23_scales:
             nc.gpsimd.memset(plane[:].bitcast(I32), 0)
         ident = keep.tile([P, P], F32, name="ident")
@@ -55,47 +57,38 @@ def tile_picked_zrandla_lin_p_kernel(
 
         w1_rows = w1.rearrange("(p j) c -> p j c", j=PACK)
         nc.sync.dma_start(out=w1_raw[0][:], in_=w1_rows[:, :, : H // 2])
-        nc.sync.dma_start(out=w1_raw[1][:], in_=w1_rows[:, :, H // 2 :])
-        load_scale_rows(nc.sync, xs, x_scales[0])
+        nc.sync.dma_start(out=xs[0:P:8, :].bitcast(I32), in_=x_scales[0].bitcast(I32))
         nc.sync.dma_start(offs_t[:], offs)
+        nc.sync.dma_start(out=w1_raw[1][:], in_=w1_rows[:, :, H // 2 :])
         nc.sync.dma_start(out=xw[:].bitcast(I32), in_=x_words[0].rearrange("p n t -> p (n t)").bitcast(I32))
         nc.sync.dma_start(out=w23_words[0][:].bitcast(I32), in_=w2_words[0].bitcast(I32))
         load_scale_rows(nc.sync, w23_scales[0], w2_scales[0])
         nc.sync.dma_start(out=w23_words[1][:].bitcast(I32), in_=w3_words[0].bitcast(I32))
-        load_scale_rows(nc.sync, w23_scales[1], w3_scales[0])
         nc.sync.dma_start(pos_t[0][:], pos1)
+        load_scale_rows(nc.sync, w23_scales[1], w3_scales[0])
         nc.sync.dma_start(pos_t[1][:], pos2)
         nc.sync.dma_start(pos_t[2][:], pos3)
 
         w1_bf = keep.tile([P, PACK * H], BF16, name="w1_bf", align_bytes=64)
         dst = w1_bf[:].rearrange("p (t m j) -> p m t j", t=PACK, j=PACK)
         src = [raw[:].rearrange("p j (m t) -> p m t j", t=PACK) for raw in w1_raw]
-        for a in range(2):
-            m0 = a * M_HALF
-            nc.scalar.copy(out=dst[:, m0 : m0 + M_SCALAR], in_=src[a][:, :M_SCALAR])
-            nc.vector.tensor_copy(out=dst[:, m0 + M_SCALAR : m0 + M_HALF], in_=src[a][:, M_SCALAR:])
+        nc.scalar.copy(out=dst[:, :M_HALF], in_=src[0])
+        picked = keep.tile([P, S], U8, name="picked", align_bytes=64)
+        nc.vector.tensor_copy(picked[:], xs[:].indirect(offs_t[:]))
+        for q in range(4):
+            nc.scalar.dma_start(
+                out=xg_scales[32 * q : 32 * q + 4, :].bitcast(I32), in_=picked[32 * q : 32 * (q + 1) : 8, :].bitcast(I32)
+            )
+
+        nc.vector.tensor_copy(out=dst[:, M_HALF:], in_=src[1])
         w1_codes = keep.tile([P, H], U32, name="w1_codes", align_bytes=64)
         w1_scales = keep.tile([P, H], U8, name="w1_scales", align_bytes=64)
         nc.vector.quantize_mx(out=w1_codes[:].bitcast(FP8X4), scales=w1_scales[:], in_=w1_bf[:])
-        xg_scales = keep.tile([P, S], U8, name="xg_scales", align_bytes=64)
-        nc.vector.tensor_copy(xg_scales[:], xs[:].indirect(offs_t[:]))
-
-        s1 = psum.tile([P, S], F32, name="s1")
-        for t in range(2):
-            nc.tensor.matmul_mx(
-                out=s1[:],
-                lhsT=w1_codes[:, t * P : (t + 1) * P].bitcast(FP8X4),
-                lhsT_scale=w1_scales[:, t * P : (t + 1) * P],
-                rhs=w1_codes[:].bitcast(FP8X4),
-                rhs_scale=w1_scales[:],
-                start=True,
-                stop=True,
-            )
 
         xg_words = []
-        for a in range(S // HALF):
-            g = keep.tile([P, HALF], U32, name=f"xg_words{a}", align_bytes=64)
-            cols = HALF // LIST_ROWS
+        for a in range(S // PIECE):
+            g = keep.tile([P, PIECE], U32, name=f"xg_words{a}", align_bytes=64)
+            cols = PIECE // LIST_ROWS
             nc.vector.tensor_copy(g[:], xw[:].indirect(offs_t[:, a * cols : (a + 1) * cols]))
             xg_words.append(g)
 
@@ -104,7 +97,7 @@ def tile_picked_zrandla_lin_p_kernel(
         h_bf = []
         for b in range(S // BLOCK):
             bank = psum.tile([P, PACK, BLOCK], F32, name=f"h_bank{b}")
-            a, o = divmod(b * BLOCK, HALF)
+            a, o = divmod(b * BLOCK, PIECE)
             for t in range(PACK):
                 cols = slice(t * P, (t + 1) * P)
                 nc.tensor.matmul_mx(
@@ -145,91 +138,69 @@ def tile_picked_zrandla_lin_p_kernel(
         last = S - BLOCK
         s0_head = psum.tile([P, last], F32, name="s0_head")
         s0_tail = psum.tile([P, BLOCK], F32, name="s0_tail")
-        y0 = psum.tile([P, S], F32, name="y0")
-        y1 = psum.tile([P, S], F32, name="y1", tag="h_bank0")
         second_product(s0_head[:, :HALF], 0, 0, slice(0, HALF))
         second_product(s0_head[:, HALF:], 0, 0, slice(HALF, last))
         nc.scalar.activation(out=e[0][:, :last], in_=s0_head[:], func=ACT.Exp)
         second_product(s0_tail[:], 0, 0, slice(last, S))
         nc.scalar.activation(out=e[0][:, last:], in_=s0_tail[:], func=ACT.Exp)
-        second_product(y0[:], 1, 0, slice(0, S))
+        s1 = psum.tile([P, S], F32, name="s1")
         second_product(s1[:], 0, 1, slice(0, S))
         nc.scalar.activation(out=e[1][:], in_=s1[:], func=ACT.Exp)
-        second_product(y1[:], 1, 1, slice(0, S))
+        y = [psum.tile([P, S], F32, name=f"y{mt}", tag=f"h_bank{mt}") for mt in range(2)]
+        for mt in range(2):
+            second_product(y[mt][:], 1, mt, slice(0, S))
 
-        def fetch(name, window, entries, prev=None, op=ALU.add, tag=None):
-            acc = keep.tile([P, LIST_ROWS * entries.shape[1]], F32, name=name, tag=tag or name)
+        def fetch(name, window, d, prev=None):
+            acc = keep.tile([P, V], F32, name=name)
             if prev is None:
-                nc.vector.tensor_copy(acc[:], window[:].indirect(entries))
+                nc.vector.tensor_copy(acc[:], window[:].indirect(pos_t[d][:]))
             else:
-                nc.vector.tensor_tensor(acc[:], window[:].indirect(entries), prev, op)
+                nc.vector.tensor_tensor(acc[:], window[:].indirect(pos_t[d][:]), prev[:], ALU.add)
             return acc
 
-        def inverse(mt, den):
-            root = keep.tile([P, V], F32, name=f"root{mt}", tag="root")
-            nc.scalar.activation(out=root[:], in_=den, func=ACT.Abs_reciprocal_sqrt)
-            inv = keep.tile([P, V], F32, name=f"inv{mt}", tag=f"inv{mt}")
-            nc.scalar.activation(out=inv[:], in_=root[:], func=ACT.Square)
-            return inv
-
-        def finish(mt, cols, total, inv):
-            res = keep.tile([P, cols.stop - cols.start], F32, name=f"res{mt}_{cols.start}")
-            nc.vector.tensor_tensor(res[:], total[:], inv[:, cols], ALU.mult)
-            nc.sync.dma_start(out=out[mt * P : (mt + 1) * P, cols], in_=res[:])
+        def fetch_scalar(name, window, d):
+            acc = keep.tile([P, V], F32, name=name)
+            nc.scalar.activation(out=acc[:], in_=window[:].indirect(pos_t[d][:]), func=ACT.Copy)
+            return acc
 
         halves = [slice(a * V // 2, (a + 1) * V // 2) for a in range(2)]
-        entries = [slice(c.start // LIST_ROWS, c.stop // LIST_ROWS) for c in halves]
 
-        def add_turned(acc, src, d):
-            nc.tensor.matmul(acc, lhsT=src, rhs=ident[:], is_transpose=True, start=(d == 0), stop=(d == 2))
+        den00 = fetch("den00", e[0], 0)
+        ye = [keep.tile([P, S], F32, name=f"ye{mt}") for mt in range(2)]
+        for mt in range(2):
+            nc.vector.tensor_tensor(ye[mt][:], y[mt][:], e[mt][:], ALU.mult)
+        e1 = [fetch_scalar(f"e1{d}", e[1], d) for d in range(3)]
+        num10 = fetch_scalar("num10", ye[1], 0)
+        den1_t = psum.tile([P, V], F32, name="den1_t", tag="h_bank1")
+        for a in range(2):
+            for d in range(3):
+                nc.tensor.matmul(
+                    den1_t[:, halves[a]],
+                    lhsT=e1[d][:, halves[a]],
+                    rhs=ident[:],
+                    is_transpose=True,
+                    start=(d == 0),
+                    stop=(d == 2),
+                )
+        num00 = fetch("num00", ye[0], 0)
+        den01 = fetch("den01", e[0], 1, den00)
+        num11 = fetch("num11", ye[1], 1, num10)
+        den02 = fetch("den02", e[0], 2, den01)
+        num01 = fetch("num01", ye[0], 1, num00)
+        num12 = fetch("num12", ye[1], 2, num11)
+        num02 = fetch("num02", ye[0], 2, num01)
 
-        y0_sb = keep.tile([P, S], F32, name="y0_sb")
-        nc.scalar.copy(out=y0_sb[:], in_=y0[:])
-        num0_t = [psum.tile([P, P], F32, name=f"num0_t{a}", tag=f"h_bank{2 + a}") for a in range(2)]
-        den0_t = psum.tile([P, V], F32, name="den0_t", tag="h_bank1")
-
-        def product(d, weights):
-            prod = fetch(f"prod0{d}", y0_sb, pos_t[d][:], weights[:], op=ALU.mult)
-            for a in range(2):
-                add_turned(num0_t[a][:], prod[:, halves[a]], d)
-
-        e00 = fetch("e00", e[0], pos_t[0][:])
-        den10 = fetch("den10", e[1], pos_t[0][:], tag="den10_then_ye1")
-        product(0, e00)
-        e01 = fetch("e01", e[0], pos_t[1][:])
-        den11 = fetch("den11", e[1], pos_t[1][:], den10[:])
-        product(1, e01)
-        e02 = fetch("e02", e[0], pos_t[2][:])
+        root1_t = keep.tile([P, V], F32, name="root1_t")
+        nc.scalar.activation(out=root1_t[:], in_=den1_t[:], func=ACT.Abs_reciprocal_sqrt)
+        root0 = keep.tile([P, V], F32, name="root0", tag="e12")
+        nc.scalar.activation(out=root0[:], in_=den02[:], func=ACT.Abs_reciprocal_sqrt)
+        root1 = psum.tile([P, V], F32, name="root1", tag="h_bank2")
         for a in range(2):
-            for d, part in enumerate((e00, e01, e02)):
-                add_turned(den0_t[:, halves[a]], part[:, halves[a]], d)
-        root0_t = keep.tile([P, V], F32, name="root0_t", tag="root")
-        nc.scalar.activation(out=root0_t[:], in_=den0_t[:], func=ACT.Abs_reciprocal_sqrt)
-        inv0_t = [keep.tile([P, P], F32, name=f"inv0_t{a}", tag=f"inv0_t{a}") for a in range(2)]
-        for a in range(2):
-            nc.scalar.activation(out=inv0_t[a][:], in_=root0_t[:, halves[a]], func=ACT.Square)
-        ye1 = keep.tile([P, S], F32, name="ye1", tag="den10_then_ye1")
-        nc.vector.tensor_tensor(ye1[:], y1[:], e[1][:], ALU.mult)
-        product(2, e02)
-        num10 = fetch("num10", ye1, pos_t[0][:])
-        den12 = fetch("den12", e[1], pos_t[2][:], den11[:])
-        inv1 = inverse(1, den12[:])
-
-        res0_t = keep.tile([P, V], F32, name="res0_t")
-        res0_back = psum.tile([P, V], F32, name="res0_back", tag="s0_head")
-        for a in range(2):
-            nc.vector.tensor_tensor(res0_t[:, halves[a]], num0_t[a][:], inv0_t[a][:], ALU.mult)
-        for a in range(2):
-            nc.tensor.transpose(res0_back[:, halves[a]], res0_t[:, halves[a]], ident[:])
-        res0 = keep.tile([P, V], F32, name="res0")
-        nc.scalar.copy(out=res0[:], in_=res0_back[:])
-        nc.sync.dma_start(out=out[:P, :], in_=res0[:])
-
-        num11 = keep.tile([P, V], F32, name="num11", tag="inv0_t0")
-        for a in range(2):
-            nc.vector.tensor_tensor(
-                num11[:, halves[a]], ye1[:].indirect(pos_t[1][:, entries[a]]), num10[:, halves[a]], ALU.add
-            )
-        num12 = [fetch(f"num12_{a}", ye1, pos_t[2][:, entries[a]], num11[:, halves[a]]) for a in range(2)]
-        for a in range(2):
-            finish(1, halves[a], num12[a], inv1)
+            nc.tensor.transpose(root1[:, halves[a]], root1_t[:, halves[a]], ident[:])
+        inv = [keep.tile([P, V], F32, name=f"inv{mt}") for mt in range(2)]
+        nc.scalar.activation(out=inv[1][:], in_=root1[:], func=ACT.Square)
+        nc.scalar.activation(out=inv[0][:], in_=root0[:], func=ACT.Square)
+        for mt, total in ((1, num12), (0, num02)):
+            res = keep.tile([P, V], F32, name=f"res{mt}")
+            nc.vector.tensor_tensor(res[:], total[:], inv[mt][:], ALU.mult)
+            nc.sync.dma_start(out=out[mt * P : (mt + 1) * P, :], in_=res[:])

@@ -1,7 +1,6 @@
 from contextlib import ExitStack
 
 import concourse.mybir as mybir
-from concourse.masks import make_identity
 
 K, T, S, V, H, N = 512, 2048, 512, 256, 512, 256
 FLOPS = 2 * K * H * S + 2 * 2 * H * N * S
@@ -21,9 +20,8 @@ P = 128
 PACK = 4
 LIST_ROWS = 16
 BLOCK = 128
-HALF = 256
-PIECE = 128
 M_HALF = P // 2
+SCORE, FEATURE = 0, 1
 
 
 def load_scale_rows(queue, plane, rows):
@@ -46,14 +44,12 @@ def tile_picked_zrandla_lin_p_kernel(
         w1_raw = [keep.tile([P, PACK, H // 2], F32, name=f"w1_raw{a}", align_bytes=64) for a in range(2)]
         w23_words = [keep.tile([P, 2 * N], U8, name=f"w23_words{i}", align_bytes=64) for i in range(2)]
         w23_scales = [keep.tile([P, N], U8, name=f"w23_scales{i}", align_bytes=64) for i in range(2)]
-
-        nc.gpsimd.memset(xs[:].bitcast(I32), 0)
         xg_scales = keep.tile([P, S], U8, name="xg_scales", align_bytes=64)
-        nc.gpsimd.memset(xg_scales[:].bitcast(I32), 0)
+
         for plane in w23_scales:
-            nc.gpsimd.memset(plane[:].bitcast(I32), 0)
-        ident = keep.tile([P, P], F32, name="ident")
-        make_identity(nc, ident[:])
+            nc.vector.memset(plane[:].bitcast(I32), 0)
+        nc.vector.memset(xs[:].bitcast(I32), 0)
+        nc.vector.memset(xg_scales[:].bitcast(I32), 0)
 
         w1_rows = w1.rearrange("(p j) c -> p j c", j=PACK)
         nc.sync.dma_start(out=w1_raw[0][:], in_=w1_rows[:, :, : H // 2])
@@ -61,13 +57,12 @@ def tile_picked_zrandla_lin_p_kernel(
         nc.sync.dma_start(offs_t[:], offs)
         nc.sync.dma_start(out=w1_raw[1][:], in_=w1_rows[:, :, H // 2 :])
         nc.sync.dma_start(out=xw[:].bitcast(I32), in_=x_words[0].rearrange("p n t -> p (n t)").bitcast(I32))
-        nc.sync.dma_start(out=w23_words[0][:].bitcast(I32), in_=w2_words[0].bitcast(I32))
-        load_scale_rows(nc.sync, w23_scales[0], w2_scales[0])
-        nc.sync.dma_start(out=w23_words[1][:].bitcast(I32), in_=w3_words[0].bitcast(I32))
-        nc.sync.dma_start(pos_t[0][:], pos1)
-        load_scale_rows(nc.sync, w23_scales[1], w3_scales[0])
-        nc.sync.dma_start(pos_t[1][:], pos2)
-        nc.sync.dma_start(pos_t[2][:], pos3)
+        nc.sync.dma_start(out=w23_words[SCORE][:].bitcast(I32), in_=w2_words[0].bitcast(I32))
+        nc.sync.dma_start(out=w23_words[FEATURE][:].bitcast(I32), in_=w3_words[0].bitcast(I32))
+        for tile, pos in zip(pos_t, (pos1, pos2, pos3)):
+            nc.sync.dma_start(tile[:], pos)
+        load_scale_rows(nc.scalar, w23_scales[SCORE], w2_scales[0])
+        load_scale_rows(nc.gpsimd, w23_scales[FEATURE], w3_scales[0])
 
         w1_bf = keep.tile([P, PACK * H], BF16, name="w1_bf", align_bytes=64)
         dst = w1_bf[:].rearrange("p (t m j) -> p m t j", t=PACK, j=PACK)
@@ -86,10 +81,10 @@ def tile_picked_zrandla_lin_p_kernel(
         nc.vector.quantize_mx(out=w1_codes[:].bitcast(FP8X4), scales=w1_scales[:], in_=w1_bf[:])
 
         xg_words = []
-        for a in range(S // PIECE):
-            g = keep.tile([P, PIECE], U32, name=f"xg_words{a}", align_bytes=64)
-            cols = PIECE // LIST_ROWS
-            nc.vector.tensor_copy(g[:], xw[:].indirect(offs_t[:, a * cols : (a + 1) * cols]))
+        for b in range(S // BLOCK):
+            g = keep.tile([P, BLOCK], U32, name=f"xg_words{b}", align_bytes=64)
+            cols = BLOCK // LIST_ROWS
+            nc.vector.tensor_copy(g[:], xw[:].indirect(offs_t[:, b * cols : (b + 1) * cols]))
             xg_words.append(g)
 
         h_codes = keep.tile([P, S], U32, name="h_codes", align_bytes=64)
@@ -97,14 +92,13 @@ def tile_picked_zrandla_lin_p_kernel(
         h_bf = []
         for b in range(S // BLOCK):
             bank = psum.tile([P, PACK, BLOCK], F32, name=f"h_bank{b}")
-            a, o = divmod(b * BLOCK, PIECE)
             for t in range(PACK):
                 cols = slice(t * P, (t + 1) * P)
                 nc.tensor.matmul_mx(
                     out=bank[:, t, :],
                     lhsT=w1_codes[:, cols].bitcast(FP8X4),
                     lhsT_scale=w1_scales[:, cols],
-                    rhs=xg_words[a][:, o : o + BLOCK].bitcast(FP8X4),
+                    rhs=xg_words[b][:].bitcast(FP8X4),
                     rhs_scale=xg_scales[:, b * BLOCK : (b + 1) * BLOCK],
                     start=True,
                     stop=True,
@@ -135,72 +129,77 @@ def tile_picked_zrandla_lin_p_kernel(
             )
 
         e = [keep.tile([P, S], F32, name=f"e{mt}") for mt in range(2)]
-        last = S - BLOCK
-        s0_head = psum.tile([P, last], F32, name="s0_head")
-        s0_tail = psum.tile([P, BLOCK], F32, name="s0_tail")
-        second_product(s0_head[:, :HALF], 0, 0, slice(0, HALF))
-        second_product(s0_head[:, HALF:], 0, 0, slice(HALF, last))
-        nc.scalar.activation(out=e[0][:, :last], in_=s0_head[:], func=ACT.Exp)
-        second_product(s0_tail[:], 0, 0, slice(last, S))
-        nc.scalar.activation(out=e[0][:, last:], in_=s0_tail[:], func=ACT.Exp)
-        s1 = psum.tile([P, S], F32, name="s1")
-        second_product(s1[:], 0, 1, slice(0, S))
-        nc.scalar.activation(out=e[1][:], in_=s1[:], func=ACT.Exp)
-        y = [psum.tile([P, S], F32, name=f"y{mt}", tag=f"h_bank{mt}") for mt in range(2)]
-        for mt in range(2):
-            second_product(y[mt][:], 1, mt, slice(0, S))
-
-        def fetch(name, window, d, prev=None):
-            acc = keep.tile([P, V], F32, name=name)
-            if prev is None:
-                nc.vector.tensor_copy(acc[:], window[:].indirect(pos_t[d][:]))
-            else:
-                nc.vector.tensor_tensor(acc[:], window[:].indirect(pos_t[d][:]), prev[:], ALU.add)
-            return acc
-
-        def fetch_scalar(name, window, d):
-            acc = keep.tile([P, V], F32, name=name)
-            nc.scalar.activation(out=acc[:], in_=window[:].indirect(pos_t[d][:]), func=ACT.Copy)
-            return acc
-
-        halves = [slice(a * V // 2, (a + 1) * V // 2) for a in range(2)]
-
-        den00 = fetch("den00", e[0], 0)
         ye = [keep.tile([P, S], F32, name=f"ye{mt}") for mt in range(2)]
-        for mt in range(2):
-            nc.vector.tensor_tensor(ye[mt][:], y[mt][:], e[mt][:], ALU.mult)
-        e1 = [fetch_scalar(f"e1{d}", e[1], d) for d in range(3)]
-        num10 = fetch_scalar("num10", ye[1], 0)
-        den1_t = psum.tile([P, V], F32, name="den1_t", tag="h_bank1")
-        for a in range(2):
-            for d in range(3):
-                nc.tensor.matmul(
-                    den1_t[:, halves[a]],
-                    lhsT=e1[d][:, halves[a]],
-                    rhs=ident[:],
-                    is_transpose=True,
-                    start=(d == 0),
-                    stop=(d == 2),
-                )
-        num00 = fetch("num00", ye[0], 0)
-        den01 = fetch("den01", e[0], 1, den00)
-        num11 = fetch("num11", ye[1], 1, num10)
-        den02 = fetch("den02", e[0], 2, den01)
-        num01 = fetch("num01", ye[0], 1, num00)
-        num12 = fetch("num12", ye[1], 2, num11)
-        num02 = fetch("num02", ye[0], 2, num01)
+        head = slice(0, 2 * BLOCK)
+        third = slice(2 * BLOCK, 3 * BLOCK)
+        last = slice(3 * BLOCK, S)
 
-        root1_t = keep.tile([P, V], F32, name="root1_t")
-        nc.scalar.activation(out=root1_t[:], in_=den1_t[:], func=ACT.Abs_reciprocal_sqrt)
-        root0 = keep.tile([P, V], F32, name="root0", tag="e12")
-        nc.scalar.activation(out=root0[:], in_=den02[:], func=ACT.Abs_reciprocal_sqrt)
-        root1 = psum.tile([P, V], F32, name="root1", tag="h_bank2")
-        for a in range(2):
-            nc.tensor.transpose(root1[:, halves[a]], root1_t[:, halves[a]], ident[:])
+        s_head = psum.tile([P, 2, 2 * BLOCK], F32, name="s_head")
+        y_head = psum.tile([P, 2, 2 * BLOCK], F32, name="y_head")
+        for mt in range(2):
+            second_product(s_head[:, mt, :], SCORE, mt, head)
+        for mt in range(2):
+            second_product(y_head[:, mt, :], FEATURE, mt, head)
+        for mt in range(2):
+            nc.scalar.activation(out=e[mt][:, head], in_=s_head[:, mt, :], func=ACT.Exp)
+        for mt in range(2):
+            nc.vector.tensor_tensor(ye[mt][:, head], y_head[:, mt, :], e[mt][:, head], ALU.mult)
+
+        s_third = psum.tile([P, 2, BLOCK], F32, name="s_third")
+        y_third = psum.tile([P, 2, BLOCK], F32, name="y_third", tag="h_bank1")
+        for mt in range(2):
+            second_product(s_third[:, mt, :], SCORE, mt, third)
+        for mt in range(2):
+            second_product(y_third[:, mt, :], FEATURE, mt, third)
+        for mt in range(2):
+            nc.scalar.activation(out=e[mt][:, third], in_=s_third[:, mt, :], func=ACT.Exp)
+        for mt in range(2):
+            nc.vector.tensor_tensor(ye[mt][:, third], y_third[:, mt, :], e[mt][:, third], ALU.mult)
+
+        s_last = [psum.tile([P, BLOCK], F32, name="s_last0"), psum.tile([P, BLOCK], F32, name="s_last1", tag="h_bank0")]
+        y_last = psum.tile([P, 2, BLOCK], F32, name="y_last", tag="h_bank2")
+        for mt in range(2):
+            second_product(s_last[mt][:], SCORE, mt, last)
+        for mt in range(2):
+            second_product(y_last[:, mt, :], FEATURE, mt, last)
+        for mt in range(2):
+            nc.scalar.activation(out=e[mt][:, last], in_=s_last[mt][:], func=ACT.Exp)
+        for mt in range(2):
+            nc.vector.tensor_tensor(ye[mt][:, last], y_last[:, mt, :], e[mt][:, last], ALU.mult)
+
+        def first_term(acc, window, cols):
+            picks = pos_t[0][:, cols.start // LIST_ROWS : cols.stop // LIST_ROWS]
+            nc.scalar.activation(out=acc[:, cols], in_=window[:].indirect(picks), func=ACT.Copy)
+
+        def add_term(acc, window, d, prev, cols):
+            picks = pos_t[d][:, cols.start // LIST_ROWS : cols.stop // LIST_ROWS]
+            nc.vector.tensor_tensor(acc[:, cols], window[:].indirect(picks), prev[:, cols], ALU.add)
+
+        whole = slice(0, V)
+        halves = [slice(0, V // 2), slice(V // 2, V)]
+        den = [[keep.tile([P, V], F32, name=f"den{mt}_{d}") for d in range(3)] for mt in range(2)]
+        num = [[keep.tile([P, V], F32, name=f"num{mt}_{d}") for d in range(3)] for mt in range(2)]
+        for cols in halves:
+            first_term(den[0][0], e[0], cols)
+        first_term(den[1][0], e[1], whole)
+        for mt in range(2):
+            first_term(num[mt][0], ye[mt], whole)
+        for cols in halves:
+            add_term(den[0][1], e[0], 1, den[0][0], cols)
+        add_term(den[1][1], e[1], 1, den[1][0], whole)
+        for mt in range(2):
+            add_term(den[mt][2], e[mt], 2, den[mt][1], whole)
+        for d in (1, 2):
+            for mt in range(2):
+                add_term(num[mt][d], ye[mt], d, num[mt][d - 1], whole)
+
+        root = [keep.tile([P, V], F32, name=f"root{mt}") for mt in range(2)]
         inv = [keep.tile([P, V], F32, name=f"inv{mt}") for mt in range(2)]
-        nc.scalar.activation(out=inv[1][:], in_=root1[:], func=ACT.Square)
-        nc.scalar.activation(out=inv[0][:], in_=root0[:], func=ACT.Square)
-        for mt, total in ((1, num12), (0, num02)):
+        for mt in range(2):
+            nc.scalar.activation(out=root[mt][:], in_=den[mt][2][:], func=ACT.Abs_reciprocal_sqrt)
+        for mt in range(2):
+            nc.scalar.activation(out=inv[mt][:], in_=root[mt][:], func=ACT.Square)
+        for mt in range(2):
             res = keep.tile([P, V], F32, name=f"res{mt}")
-            nc.vector.tensor_tensor(res[:], total[:], inv[mt][:], ALU.mult)
+            nc.vector.tensor_tensor(res[:], num[mt][2][:], inv[mt][:], ALU.mult)
             nc.sync.dma_start(out=out[mt * P : (mt + 1) * P, :], in_=res[:])

@@ -20,7 +20,7 @@ P = 128
 PACK = 4
 LIST_ROWS = 16
 BLOCK = 128
-M_HALF = P // 2
+SCALAR_GROUPS = 44
 SCORE, FEATURE = 0, 1
 
 
@@ -41,21 +41,24 @@ def tile_picked_zrandla_lin_p_kernel(
         pos_t = [keep.tile([P, V // LIST_ROWS], U16, name=f"pos_t{d}") for d in range(3)]
         xw = keep.tile([P, T], U32, name="xw", align_bytes=64)
         xs = keep.tile([P, T], U8, name="xs", align_bytes=64)
-        w1_raw = [keep.tile([P, PACK, H // 2], F32, name=f"w1_raw{a}", align_bytes=64) for a in range(2)]
+        w1_raw = keep.tile([P, PACK, H], F32, name="w1_raw", align_bytes=64)
         w23_words = [keep.tile([P, 2 * N], U8, name=f"w23_words{i}", align_bytes=64) for i in range(2)]
         w23_scales = [keep.tile([P, N], U8, name=f"w23_scales{i}", align_bytes=64) for i in range(2)]
         xg_scales = keep.tile([P, S], U8, name="xg_scales", align_bytes=64)
 
+        nc.vector.memset(xs[:].bitcast(I32), 0)
+        warm = keep.tile([P, 2], F32, name="warm")
+        nc.gpsimd.memset(warm[:, 0:1], 0.0)
+        nc.scalar.activation(out=warm[:, 1:2], in_=warm[:, 0:1], func=ACT.Exp)
         for plane in w23_scales:
             nc.vector.memset(plane[:].bitcast(I32), 0)
-        nc.vector.memset(xs[:].bitcast(I32), 0)
         nc.vector.memset(xg_scales[:].bitcast(I32), 0)
 
         w1_rows = w1.rearrange("(p j) c -> p j c", j=PACK)
-        nc.sync.dma_start(out=w1_raw[0][:], in_=w1_rows[:, :, : H // 2])
+        nc.sync.dma_start(out=w1_raw[:, :1, :], in_=w1_rows[:, :1, :])
         nc.sync.dma_start(out=xs[0:P:8, :].bitcast(I32), in_=x_scales[0].bitcast(I32))
         nc.sync.dma_start(offs_t[:], offs)
-        nc.sync.dma_start(out=w1_raw[1][:], in_=w1_rows[:, :, H // 2 :])
+        nc.sync.dma_start(out=w1_raw[:, 1:, :], in_=w1_rows[:, 1:, :])
         nc.sync.dma_start(out=xw[:].bitcast(I32), in_=x_words[0].rearrange("p n t -> p (n t)").bitcast(I32))
         nc.sync.dma_start(out=w23_words[SCORE][:].bitcast(I32), in_=w2_words[0].bitcast(I32))
         nc.sync.dma_start(out=w23_words[FEATURE][:].bitcast(I32), in_=w3_words[0].bitcast(I32))
@@ -66,8 +69,7 @@ def tile_picked_zrandla_lin_p_kernel(
 
         w1_bf = keep.tile([P, PACK * H], BF16, name="w1_bf", align_bytes=64)
         dst = w1_bf[:].rearrange("p (t m j) -> p m t j", t=PACK, j=PACK)
-        src = [raw[:].rearrange("p j (m t) -> p m t j", t=PACK) for raw in w1_raw]
-        nc.scalar.copy(out=dst[:, :M_HALF], in_=src[0])
+        src = w1_raw[:].rearrange("p j (m t) -> p m t j", t=PACK)
         picked = keep.tile([P, S], U8, name="picked", align_bytes=64)
         nc.vector.tensor_copy(picked[:], xs[:].indirect(offs_t[:]))
         for q in range(4):
@@ -75,7 +77,8 @@ def tile_picked_zrandla_lin_p_kernel(
                 out=xg_scales[32 * q : 32 * q + 4, :].bitcast(I32), in_=picked[32 * q : 32 * (q + 1) : 8, :].bitcast(I32)
             )
 
-        nc.vector.tensor_copy(out=dst[:, M_HALF:], in_=src[1])
+        nc.scalar.copy(out=dst[:, :SCALAR_GROUPS], in_=src[:, :SCALAR_GROUPS])
+        nc.vector.tensor_copy(out=dst[:, SCALAR_GROUPS:], in_=src[:, SCALAR_GROUPS:])
         w1_codes = keep.tile([P, H], U32, name="w1_codes", align_bytes=64)
         w1_scales = keep.tile([P, H], U8, name="w1_scales", align_bytes=64)
         nc.vector.quantize_mx(out=w1_codes[:].bitcast(FP8X4), scales=w1_scales[:], in_=w1_bf[:])

@@ -187,14 +187,20 @@ def tile_picked_zrandla_lin_p_kernel(
         first_term(den[1][0], e[1], whole)
         for mt in range(2):
             first_term(num[mt][0], ye[mt], whole)
+        extra = keep.tile([P, V // 2], F32, name="extra")
+        nc.scalar.activation(
+            out=extra[:], in_=ye[1][:].indirect(pos_t[2][:, V // 2 // LIST_ROWS :]), func=ACT.Copy
+        )
         for cols in halves:
             add_term(den[0][1], e[0], 1, den[0][0], cols)
         add_term(den[1][1], e[1], 1, den[1][0], whole)
         for mt in range(2):
             add_term(den[mt][2], e[mt], 2, den[mt][1], whole)
-        for d in (1, 2):
-            for mt in range(2):
-                add_term(num[mt][d], ye[mt], d, num[mt][d - 1], whole)
+        for mt in range(2):
+            add_term(num[mt][1], ye[mt], 1, num[mt][0], whole)
+        add_term(num[0][2], ye[0], 2, num[0][1], whole)
+        add_term(num[1][2], ye[1], 2, num[1][1], halves[0])
+        nc.vector.tensor_tensor(num[1][2][:, halves[1]], num[1][1][:, halves[1]], extra[:], ALU.add)
 
         root = [keep.tile([P, V], F32, name=f"root{mt}") for mt in range(2)]
         inv = [keep.tile([P, V], F32, name=f"inv{mt}") for mt in range(2)]
@@ -204,5 +210,6 @@ def tile_picked_zrandla_lin_p_kernel(
             nc.scalar.activation(out=inv[mt][:], in_=root[mt][:], func=ACT.Square)
         for mt in range(2):
             res = keep.tile([P, V], F32, name=f"res{mt}")
-            nc.vector.tensor_tensor(res[:], num[mt][2][:], inv[mt][:], ALU.mult)
-            nc.sync.dma_start(out=out[mt * P : (mt + 1) * P, :], in_=res[:])
+            for cols in halves if mt else [whole]:
+                nc.vector.tensor_tensor(res[:, cols], num[mt][2][:, cols], inv[mt][:, cols], ALU.mult)
+                nc.sync.dma_start(out=out[mt * P : (mt + 1) * P, cols], in_=res[:, cols])

@@ -20,7 +20,7 @@ P = 128
 PACK = 4
 LIST_ROWS = 16
 BLOCK = 128
-SCALAR_GROUPS = 44
+SCALAR_GROUPS = 30
 SCORE, FEATURE = 0, 1
 
 
@@ -50,14 +50,14 @@ def tile_picked_zrandla_lin_p_kernel(
         warm = keep.tile([P, 2], F32, name="warm")
         nc.gpsimd.memset(warm[:, 0:1], 0.0)
         nc.scalar.activation(out=warm[:, 1:2], in_=warm[:, 0:1], func=ACT.Exp)
-        for plane in w23_scales:
-            nc.vector.memset(plane[:].bitcast(I32), 0)
+        nc.gpsimd.memset(w23_scales[FEATURE][:].bitcast(I32), 0)
+        nc.vector.memset(w23_scales[SCORE][:].bitcast(I32), 0)
         nc.vector.memset(xg_scales[:].bitcast(I32), 0)
 
         w1_rows = w1.rearrange("(p j) c -> p j c", j=PACK)
         nc.sync.dma_start(out=w1_raw[:, :1, :], in_=w1_rows[:, :1, :])
-        nc.sync.dma_start(out=xs[0:P:8, :].bitcast(I32), in_=x_scales[0].bitcast(I32))
         nc.sync.dma_start(offs_t[:], offs)
+        nc.sync.dma_start(out=xs[0:P:8, :].bitcast(I32), in_=x_scales[0].bitcast(I32))
         nc.sync.dma_start(out=w1_raw[:, 1:, :], in_=w1_rows[:, 1:, :])
         nc.sync.dma_start(out=xw[:].bitcast(I32), in_=x_words[0].rearrange("p n t -> p (n t)").bitcast(I32))
         nc.sync.dma_start(out=w23_words[SCORE][:].bitcast(I32), in_=w2_words[0].bitcast(I32))
@@ -81,7 +81,12 @@ def tile_picked_zrandla_lin_p_kernel(
         nc.vector.tensor_copy(out=dst[:, SCALAR_GROUPS:], in_=src[:, SCALAR_GROUPS:])
         w1_codes = keep.tile([P, H], U32, name="w1_codes", align_bytes=64)
         w1_scales = keep.tile([P, H], U8, name="w1_scales", align_bytes=64)
-        nc.vector.quantize_mx(out=w1_codes[:].bitcast(FP8X4), scales=w1_scales[:], in_=w1_bf[:])
+        for cols in (slice(0, P), slice(P, H)):
+            nc.vector.quantize_mx(
+                out=w1_codes[:, cols].bitcast(FP8X4),
+                scales=w1_scales[:, cols],
+                in_=w1_bf[:, PACK * cols.start : PACK * cols.stop],
+            )
 
         xg_words = []
         for b in range(S // BLOCK):

@@ -21,6 +21,8 @@ PACK = 4
 LIST_ROWS = 16
 BLOCK = 128
 SCALAR_GROUPS = 30
+SPREAD_FROM = 4
+PLANE_FROM = 8
 SCORE, FEATURE = 0, 1
 
 
@@ -57,7 +59,7 @@ def tile_picked_zrandla_lin_p_kernel(
         w1_rows = w1.rearrange("(p j) c -> p j c", j=PACK)
         nc.sync.dma_start(out=w1_raw[:, :1, :], in_=w1_rows[:, :1, :])
         nc.sync.dma_start(offs_t[:], offs)
-        nc.sync.dma_start(out=xs[0:P:8, :].bitcast(I32), in_=x_scales[0].bitcast(I32))
+        nc.sync.dma_start(out=xs[SPREAD_FROM:P:8, :].bitcast(I32), in_=x_scales[0].bitcast(I32))
         nc.sync.dma_start(out=w1_raw[:, 1:, :], in_=w1_rows[:, 1:, :])
         nc.sync.dma_start(out=xw[:].bitcast(I32), in_=x_words[0].rearrange("p n t -> p (n t)").bitcast(I32))
         nc.sync.dma_start(out=w23_words[SCORE][:].bitcast(I32), in_=w2_words[0].bitcast(I32))
@@ -74,7 +76,8 @@ def tile_picked_zrandla_lin_p_kernel(
         nc.vector.tensor_copy(picked[:], xs[:].indirect(offs_t[:]))
         for q in range(4):
             nc.scalar.dma_start(
-                out=xg_scales[32 * q : 32 * q + 4, :].bitcast(I32), in_=picked[32 * q : 32 * (q + 1) : 8, :].bitcast(I32)
+                out=xg_scales[32 * q + PLANE_FROM : 32 * q + PLANE_FROM + 4, :].bitcast(I32),
+                in_=picked[32 * q + SPREAD_FROM : 32 * (q + 1) : 8, :].bitcast(I32),
             )
 
         nc.scalar.copy(out=dst[:, :SCALAR_GROUPS], in_=src[:, :SCALAR_GROUPS])
@@ -107,7 +110,7 @@ def tile_picked_zrandla_lin_p_kernel(
                     lhsT=w1_codes[:, cols].bitcast(FP8X4),
                     lhsT_scale=w1_scales[:, cols],
                     rhs=xg_words[b][:].bitcast(FP8X4),
-                    rhs_scale=xg_scales[:, b * BLOCK : (b + 1) * BLOCK],
+                    rhs_scale=xg_scales[PLANE_FROM:P, b * BLOCK : (b + 1) * BLOCK],
                     start=True,
                     stop=True,
                 )
@@ -196,13 +199,13 @@ def tile_picked_zrandla_lin_p_kernel(
         nc.scalar.activation(
             out=extra[:], in_=ye[1][:].indirect(pos_t[2][:, V // 2 // LIST_ROWS :]), func=ACT.Copy
         )
-        for cols in halves:
-            add_term(den[0][1], e[0], 1, den[0][0], cols)
+        for d in (1, 2):
+            for cols in halves:
+                add_term(den[0][d], e[0], d, den[0][d - 1], cols)
         add_term(den[1][1], e[1], 1, den[1][0], whole)
-        for mt in range(2):
-            add_term(den[mt][2], e[mt], 2, den[mt][1], whole)
-        for mt in range(2):
-            add_term(num[mt][1], ye[mt], 1, num[mt][0], whole)
+        add_term(num[0][1], ye[0], 1, num[0][0], whole)
+        add_term(den[1][2], e[1], 2, den[1][1], whole)
+        add_term(num[1][1], ye[1], 1, num[1][0], whole)
         add_term(num[0][2], ye[0], 2, num[0][1], whole)
         add_term(num[1][2], ye[1], 2, num[1][1], halves[0])
         nc.vector.tensor_tensor(num[1][2][:, halves[1]], num[1][1][:, halves[1]], extra[:], ALU.add)
@@ -212,7 +215,8 @@ def tile_picked_zrandla_lin_p_kernel(
         for mt in range(2):
             nc.scalar.activation(out=root[mt][:], in_=den[mt][2][:], func=ACT.Abs_reciprocal_sqrt)
         for mt in range(2):
-            nc.scalar.activation(out=inv[mt][:], in_=root[mt][:], func=ACT.Square)
+            for cols in halves if mt else [whole]:
+                nc.scalar.activation(out=inv[mt][:, cols], in_=root[mt][:, cols], func=ACT.Square)
         for mt in range(2):
             res = keep.tile([P, V], F32, name=f"res{mt}")
             for cols in halves if mt else [whole]:

@@ -70,8 +70,8 @@ def tile_picked_zrandla_lin_p_kernel(
         load_scale_rows(nc.gpsimd, w23_scales[FEATURE], w3_scales[0])
 
         w1_bf = keep.tile([P, PACK * H], BF16, name="w1_bf", align_bytes=64)
-        dst = w1_bf[:].rearrange("p (t m j) -> p m t j", t=PACK, j=PACK)
-        src = w1_raw[:].rearrange("p j (m t) -> p m t j", t=PACK)
+        dst = w1_bf[:].rearrange("p (t m j) -> p m j t", t=PACK, j=PACK)
+        src = w1_raw[:].rearrange("p j (m t) -> p m j t", t=PACK)
         picked = keep.tile([P, S], U8, name="picked", align_bytes=64)
         nc.vector.tensor_copy(picked[:], xs[:].indirect(offs_t[:]))
         for q in range(4):

from contextlib import ExitStack

import concourse.mybir as mybir

K, T, S, V, H, N = 512, 2048, 512, 256, 512, 256
FLOPS = 2 * K * H * S + 2 * 2 * H * N * S

F32 = mybir.dt.float32
BF16 = mybir.dt.bfloat16
I32 = mybir.dt.int32
U32 = mybir.dt.uint32
U16 = mybir.dt.uint16
U8 = mybir.dt.uint8
FP8X4 = mybir.dt.float8_e4m3fn_x4
FP4X4 = mybir.dt.float4_e2m1fn_x4
ACT = mybir.ActivationFunctionType
ALU = mybir.AluOpType

P = 128
PACK = 4
LIST_ROWS = 16
BLOCK = 128
SCALAR_GROUPS = 30
SPREAD_FROM = 4
PLANE_FROM = 8
SCORE, FEATURE = 0, 1


def load_scale_rows(queue, plane, rows):
    for q in range(4):
        queue.dma_start(out=plane[32 * q : 32 * q + 4, :].bitcast(I32), in_=rows[4 * q : 4 * q + 4, :].bitcast(I32))


def tile_picked_zrandla_lin_p_kernel(
    tc, x_words, x_scales, w1, w2_words, w2_scales, w3_words, w3_scales, offs, pos1, pos2, pos3, out
):
    nc = tc.nc
    with ExitStack() as ctx:
        keep = ctx.enter_context(tc.tile_pool(name="keep", bufs=1))
        psum = ctx.enter_context(tc.psum_pool(name="psum", bufs=1))

        offs_t = keep.tile([P, S // LIST_ROWS], U16, name="offs_t")
        pos_t = [keep.tile([P, V // LIST_ROWS], U16, name=f"pos_t{d}") for d in range(3)]
        xw = keep.tile([P, T], U32, name="xw", align_bytes=64)
        xs = keep.tile([P, T], U8, name="xs", align_bytes=64)
        w1_raw = keep.tile([P, PACK, H], F32, name="w1_raw", align_bytes=64)
        w23_words = [keep.tile([P, 2 * N], U8, name=f"w23_words{i}", align_bytes=64) for i in range(2)]
        w23_scales = [keep.tile([P, N], U8, name=f"w23_scales{i}", align_bytes=64) for i in range(2)]
        xg_scales = keep.tile([P, S], U8, name="xg_scales", align_bytes=64)

        nc.vector.memset(xs[:].bitcast(I32), 0)
        warm = keep.tile([P, 2], F32, name="warm")
        nc.gpsimd.memset(warm[:, 0:1], 0.0)
        nc.scalar.activation(out=warm[:, 1:2], in_=warm[:, 0:1], func=ACT.Exp)
        nc.gpsimd.memset(w23_scales[FEATURE][:].bitcast(I32), 0)
        nc.vector.memset(w23_scales[SCORE][:].bitcast(I32), 0)
        nc.vector.memset(xg_scales[:].bitcast(I32), 0)

        w1_rows = w1.rearrange("(p j) c -> p j c", j=PACK)
        nc.sync.dma_start(out=w1_raw[:, :1, :], in_=w1_rows[:, :1, :])
        nc.sync.dma_start(offs_t[:], offs)
        nc.sync.dma_start(out=xs[SPREAD_FROM:P:8, :].bitcast(I32), in_=x_scales[0].bitcast(I32))
        nc.sync.dma_start(out=w1_raw[:, 1:, :], in_=w1_rows[:, 1:, :])
        nc.sync.dma_start(out=xw[:].bitcast(I32), in_=x_words[0].rearrange("p n t -> p (n t)").bitcast(I32))
        nc.sync.dma_start(out=w23_words[SCORE][:].bitcast(I32), in_=w2_words[0].bitcast(I32))
        nc.sync.dma_start(out=w23_words[FEATURE][:].bitcast(I32), in_=w3_words[0].bitcast(I32))
        for tile, pos in zip(pos_t, (pos1, pos2, pos3)):
            nc.sync.dma_start(tile[:], pos)
        load_scale_rows(nc.scalar, w23_scales[SCORE], w2_scales[0])
        load_scale_rows(nc.gpsimd, w23_scales[FEATURE], w3_scales[0])

        w1_bf = keep.tile([P, PACK * H], BF16, name="w1_bf", align_bytes=64)
        dst = w1_bf[:].rearrange("p (t m j) -> p m j t", t=PACK, j=PACK)
        src = w1_raw[:].rearrange("p j (m t) -> p m j t", t=PACK)
        picked = keep.tile([P, S], U8, name="picked", align_bytes=64)
        nc.vector.tensor_copy(picked[:], xs[:].indirect(offs_t[:]))
        for q in range(4):
            nc.scalar.dma_start(
                out=xg_scales[32 * q + PLANE_FROM : 32 * q + PLANE_FROM + 4, :].bitcast(I32),
                in_=picked[32 * q + SPREAD_FROM : 32 * (q + 1) : 8, :].bitcast(I32),
            )

        nc.scalar.copy(out=dst[:, :SCALAR_GROUPS], in_=src[:, :SCALAR_GROUPS])
        nc.vector.tensor_copy(out=dst[:, SCALAR_GROUPS:], in_=src[:, SCALAR_GROUPS:])
        w1_codes = keep.tile([P, H], U32, name="w1_codes", align_bytes=64)
        w1_scales = keep.tile([P, H], U8, name="w1_scales", align_bytes=64)
        for cols in (slice(0, P), slice(P, H)):
            nc.vector.quantize_mx(
                out=w1_codes[:, cols].bitcast(FP8X4),
                scales=w1_scales[:, cols],
                in_=w1_bf[:, PACK * cols.start : PACK * cols.stop],
            )

        xg_words = []
        for b in range(S // BLOCK):
            g = keep.tile([P, BLOCK], U32, name=f"xg_words{b}", align_bytes=64)
            cols = BLOCK // LIST_ROWS
            nc.vector.tensor_copy(g[:], xw[:].indirect(offs_t[:, b * cols : (b + 1) * cols]))
            xg_words.append(g)

        h_codes = keep.tile([P, S], U32, name="h_codes", align_bytes=64)
        h_scales = keep.tile([P, S], U8, name="h_scales", align_bytes=64)
        h_bf = []
        for b in range(S // BLOCK):
            bank = psum.tile([P, PACK, BLOCK], F32, name=f"h_bank{b}")
            for t in range(PACK):
                cols = slice(t * P, (t + 1) * P)
                nc.tensor.matmul_mx(
                    out=bank[:, t, :],
                    lhsT=w1_codes[:, cols].bitcast(FP8X4),
                    lhsT_scale=w1_scales[:, cols],
                    rhs=xg_words[b][:].bitcast(FP8X4),
                    rhs_scale=xg_scales[PLANE_FROM:P, b * BLOCK : (b + 1) * BLOCK],
                    start=True,
                    stop=True,
                )
            hb = keep.tile([P, BLOCK, PACK], BF16, name=f"h_bf{b}", align_bytes=64)
            if b != 1:
                nc.scalar.copy(out=hb[:], in_=bank[:].rearrange("p t n -> p n t"))
            else:
                nc.vector.tensor_copy(out=hb[:], in_=bank[:].rearrange("p t n -> p n t"))
            h_bf.append(hb)
        for b in range(S // BLOCK):
            cols = slice(b * BLOCK, (b + 1) * BLOCK)
            nc.vector.quantize_mx(
                out=h_codes[:, cols].bitcast(FP8X4),
                scales=h_scales[:, cols],
                in_=h_bf[b][:].rearrange("p n t -> p (n t)"),
            )

        def second_product(acc, which, mt, cols):
            nc.tensor.matmul_mx(
                out=acc,
                lhsT=w23_words[which][:, 2 * P * mt : 2 * P * (mt + 1)].bitcast(FP4X4),
                lhsT_scale=w23_scales[which][:, P * mt : P * (mt + 1)],
                rhs=h_codes[:, cols].bitcast(FP8X4),
                rhs_scale=h_scales[:, cols],
                start=True,
                stop=True,
            )

        e = [keep.tile([P, S], F32, name=f"e{mt}") for mt in range(2)]
        ye = [keep.tile([P, S], F32, name=f"ye{mt}") for mt in range(2)]
        head = slice(0, 2 * BLOCK)
        third = slice(2 * BLOCK, 3 * BLOCK)
        last = slice(3 * BLOCK, S)

        s_head = psum.tile([P, 2, 2 * BLOCK], F32, name="s_head")
        y_head = psum.tile([P, 2, 2 * BLOCK], F32, name="y_head")
        for mt in range(2):
            second_product(s_head[:, mt, :], SCORE, mt, head)
        for mt in range(2):
            second_product(y_head[:, mt, :], FEATURE, mt, head)
        for mt in range(2):
            nc.scalar.activation(out=e[mt][:, head], in_=s_head[:, mt, :], func=ACT.Exp)
        for mt in range(2):
            nc.vector.tensor_tensor(ye[mt][:, head], y_head[:, mt, :], e[mt][:, head], ALU.mult)

        s_third = psum.tile([P, 2, BLOCK], F32, name="s_third")
        y_third = psum.tile([P, 2, BLOCK], F32, name="y_third", tag="h_bank1")
        for mt in range(2):
            second_product(s_third[:, mt, :], SCORE, mt, third)
        for mt in range(2):
            second_product(y_third[:, mt, :], FEATURE, mt, third)
        for mt in range(2):
            nc.scalar.activation(out=e[mt][:, third], in_=s_third[:, mt, :], func=ACT.Exp)
        for mt in range(2):
            nc.vector.tensor_tensor(ye[mt][:, third], y_third[:, mt, :], e[mt][:, third], ALU.mult)

        s_last = [psum.tile([P, BLOCK], F32, name="s_last0"), psum.tile([P, BLOCK], F32, name="s_last1", tag="h_bank0")]
        y_last = psum.tile([P, 2, BLOCK], F32, name="y_last", tag="h_bank2")
        for mt in range(2):
            second_product(s_last[mt][:], SCORE, mt, last)
        for mt in range(2):
            second_product(y_last[:, mt, :], FEATURE, mt, last)
        for mt in range(2):
            nc.scalar.activation(out=e[mt][:, last], in_=s_last[mt][:], func=ACT.Exp)
        for mt in range(2):
            nc.vector.tensor_tensor(ye[mt][:, last], y_last[:, mt, :], e[mt][:, last], ALU.mult)

        def first_term(acc, window, cols):
            picks = pos_t[0][:, cols.start // LIST_ROWS : cols.stop // LIST_ROWS]
            nc.scalar.activation(out=acc[:, cols], in_=window[:].indirect(picks), func=ACT.Copy)

        def add_term(acc, window, d, prev, cols):
            picks = pos_t[d][:, cols.start // LIST_ROWS : cols.stop // LIST_ROWS]
            nc.vector.tensor_tensor(acc[:, cols], window[:].indirect(picks), prev[:, cols], ALU.add)

        whole = slice(0, V)
        halves = [slice(0, V // 2), slice(V // 2, V)]
        den = [[keep.tile([P, V], F32, name=f"den{mt}_{d}") for d in range(3)] for mt in range(2)]
        num = [[keep.tile([P, V], F32, name=f"num{mt}_{d}") for d in range(3)] for mt in range(2)]
        for cols in halves:
            first_term(den[0][0], e[0], cols)
        first_term(den[1][0], e[1], whole)
        for mt in range(2):
            first_term(num[mt][0], ye[mt], whole)
        extra = keep.tile([P, V // 2], F32, name="extra")
        nc.scalar.activation(
            out=extra[:], in_=ye[1][:].indirect(pos_t[2][:, V // 2 // LIST_ROWS :]), func=ACT.Copy
        )
        for d in (1, 2):
            for cols in halves:
                add_term(den[0][d], e[0], d, den[0][d - 1], cols)
        add_term(den[1][1], e[1], 1, den[1][0], whole)
        add_term(num[0][1], ye[0], 1, num[0][0], whole)
        add_term(den[1][2], e[1], 2, den[1][1], whole)
        add_term(num[1][1], ye[1], 1, num[1][0], whole)
        add_term(num[0][2], ye[0], 2, num[0][1], whole)
        add_term(num[1][2], ye[1], 2, num[1][1], halves[0])
        nc.vector.tensor_tensor(num[1][2][:, halves[1]], num[1][1][:, halves[1]], extra[:], ALU.add)

        root = [keep.tile([P, V], F32, name=f"root{mt}") for mt in range(2)]
        inv = [keep.tile([P, V], F32, name=f"inv{mt}") for mt in range(2)]
        for mt in range(2):
            nc.scalar.activation(out=root[mt][:], in_=den[mt][2][:], func=ACT.Abs_reciprocal_sqrt)
        for mt in range(2):
            for cols in halves if mt else [whole]:
                nc.scalar.activation(out=inv[mt][:, cols], in_=root[mt][:, cols], func=ACT.Square)
        for mt in range(2):
            res = keep.tile([P, V], F32, name=f"res{mt}")
            for cols in halves if mt else [whole]:
                nc.vector.tensor_tensor(res[:, cols], num[mt][2][:, cols], inv[mt][:, cols], ALU.mult)
                nc.sync.dma_start(out=out[mt * P : (mt + 1) * P, cols], in_=res[:, cols])
